import numpy as np
import ml_dtypes


def mxq(x, axis, fmt="e4m3"):
    dtype, down = {"e4m3": (ml_dtypes.float8_e4m3fn, 7), "e5m2": (ml_dtypes.float8_e5m2, 14)}[fmt]
    v = np.moveaxis(np.asarray(x, np.float32).astype(ml_dtypes.bfloat16).astype(np.float64), axis, -1)
    blocks = v.reshape(v.shape[:-1] + (-1, 32))
    amax = np.abs(blocks).max(-1, keepdims=True)
    byte = np.maximum(np.where(amax > 0, np.frexp(amax)[1] - 1 + 127, 0) - down, 1)
    scale = np.exp2(byte - 127.0)
    codes = (blocks / scale).astype(np.float32).astype(dtype).astype(np.float64)
    return np.moveaxis((codes * scale).reshape(v.shape), -1, axis)


WIDE = False


def mx_kscale(k):
    if not WIDE:
        return np.ones(k)
    levels = np.array([10, -10, 5, -5, 0])
    if k % 512:
        return np.exp2(np.random.permutation(np.resize(levels, k // 32))).repeat(32)
    a = np.empty((k // 512, 16))
    for p in range(k // 512):
        a[p, :8] = np.random.permutation(np.resize(levels, 8))
        for g in range(8):
            far = levels[np.abs(levels - a[p, g]) >= 10]
            a[p, g + 8] = far[np.random.randint(len(far))]
    return np.exp2(a.ravel()).repeat(32)


def f64(x):
    return np.asarray(x).astype(np.float64)


def striped(idx):
    return np.tile(np.asarray(idx).reshape(-1, 16).T, (8, 1)).astype(np.uint16)


def unstriped(offs):
    return offs[:16].T.reshape(-1).astype(np.int64)


def striped8(idx):
    return np.asarray(idx).reshape(8, -1, 16).transpose(0, 2, 1).reshape(128, -1).astype(np.uint16)


def unstriped8(offs):
    return offs.reshape(8, 16, -1).transpose(0, 2, 1).reshape(8, -1).astype(np.int64)


def pick8(x, idx, run):
    r = np.arange(len(x))
    return x[r[:, None], idx[r % (8 * run) // run]]


E2M1 = np.array([0.0, 0.5, 1.0, 1.5, 2.0, 3.0, 4.0, 6.0, -0.0, -0.5, -1.0, -1.5, -2.0, -3.0, -4.0, -6.0])


def pack_weight(w, fmt):
    k, n = w.shape
    w = f64(np.asarray(w, np.float32).astype(ml_dtypes.bfloat16)).reshape(k // 32, 32, n)
    amax = np.abs(w).max(1)
    if fmt == "e4m3":
        byte = np.frexp(amax)[1] - 1 + 127 - 7
    else:
        mant, ex = np.frexp(amax / 6.0)
        byte = np.where(mant > 0.5, ex, ex - 1) + 127
    byte = np.clip(np.where(amax > 0, byte, 1), 1, 254)
    scaled = (w * np.exp2(127.0 - byte)[:, None, :]).reshape(k, n).astype(np.float32)
    by_word = np.ascontiguousarray(scaled.reshape(k // 512, 128, 4, n).transpose(0, 1, 3, 2))
    if fmt == "e4m3":
        words = by_word.astype(ml_dtypes.float8_e4m3fn).view(np.uint8)
    else:
        c = by_word.astype(ml_dtypes.float4_e2m1fn).view(np.uint8) & 0xF
        words = (c[..., 0::2] | (c[..., 1::2] << 4)).reshape(k // 512, 128, 2 * n)
    return np.ascontiguousarray(words), np.ascontiguousarray(byte.astype(np.uint8).reshape(k // 512, 16, n))


def unpack_weight(words, scales, fmt):
    g, _, n = scales.shape
    words = np.ascontiguousarray(words).reshape(g, 128, n, -1)
    if fmt == "e4m3":
        vals = words.view(ml_dtypes.float8_e4m3fn).astype(np.float64)
    else:
        nib = np.empty((g, 128, n, 4), np.uint8)
        nib[..., 0::2] = words & 0xF
        nib[..., 1::2] = words >> 4
        vals = E2M1[nib]
    vals = vals * np.repeat(np.exp2(scales.astype(np.float64) - 127.0), 8, axis=1)[..., None]
    return vals.transpose(0, 1, 3, 2).reshape(g * 512, n)


def sgn(shape):
    return np.random.uniform(0.5, 2.0, shape) * np.where(np.random.standard_normal(shape) < 0, -1.0, 1.0)


K, J, R, T, U, F, S, O, N, Z, W = 512, 512, 512, 1024, 1024, 1024, 256, 128, 256, 512, 512


def setup_inputs():
    n = np.random.standard_normal
    idx = np.stack([np.random.permutation(T)[:J] for _ in range(8)])
    idx2 = np.stack([np.random.permutation(U)[:J] for _ in range(8)])
    idx3 = np.random.permutation(F)[:R]
    idx4 = np.stack([np.random.permutation(J)[:S] for _ in range(8)])
    idx5 = np.random.permutation(J)[:S]
    idx6 = np.stack([np.random.permutation(Z)[:N] for _ in range(8)])
    idx7 = np.stack([np.random.permutation(W)[:N] for _ in range(8)])
    fk = mx_kscale(K)
    fr = mx_kscale(R)
    tr = np.ones(F)
    tr[idx3] = fr
    wtp = pack_weight(n((K, F)) * 1 / np.sqrt(K) / fk[:, None] * tr, "e4m3")
    return {
        "ta": (np.random.randint(-7, 8, (K, T)).astype(np.float64)).astype(np.float32),
        "tb": (np.random.randint(-7, 8, (K, U)).astype(np.float64)).astype(np.float32),
        "ga": ((np.random.randint(8, 25, (K, 1)) / 64.0) * fk[:, None]).astype(np.float32),
        "gb": ((np.random.randint(8, 25, (K, 1)) / 64.0) * fk[:, None]).astype(np.float32),
        "wt_words": wtp[0],
        "wt_scales": wtp[1],
        "sa": (sgn((R, 1))).astype(np.float32),
        "sb": (sgn((R, 1))).astype(np.float32),
        "va": (np.random.randint(-7, 8, (R, Z)).astype(np.float64)).astype(np.float32),
        "vb": (np.random.randint(-7, 8, (R, W)).astype(np.float64)).astype(np.float32),
        "ea": ((np.random.randint(10, 25, (R, 1)) / 1024.0) / fr[:, None]).astype(np.float32),
        "eb": ((np.random.randint(4, 13, (R, 1)) / 1024.0) / fr[:, None]).astype(np.float32),
        "offs": striped8(idx),
        "offs2": striped8(idx2),
        "offs3": striped(idx3),
        "offs4": striped8(idx4),
        "offs5": striped(idx5),
        "offs6": striped8(idx6),
        "offs7": striped8(idx7),
    }


def reference(ta, tb, ga, gb, wt_words, wt_scales, sa, sb, va, vb, ea, eb, offs, offs2, offs3, offs4, offs5, offs6, offs7):
    idx = unstriped8(offs)
    idx2 = unstriped8(offs2)
    idx3 = unstriped(offs3)
    idx4 = unstriped8(offs4)
    idx5 = unstriped(offs5)
    idx6 = unstriped8(offs6)
    idx7 = unstriped8(offs7)
    wtu = unpack_weight(wt_words, wt_scales, "e4m3")
    xc = np.maximum(pick8(f64(ta), idx, 64) * f64(ga), pick8(f64(tb), idx2, 64) * f64(gb))
    wtidx3g = wtu[:, idx3]
    xcq = mxq(xc, 0, "e4m3")
    a = wtidx3g.T @ xcq
    h1 = np.maximum(pick8(a, idx4, 64) * f64(sa), a[:, idx5] * f64(sb))
    hid = h1.reshape(R, O, S // O).max(axis=2)
    vc = pick8(f64(va), idx6, 64) * f64(ea) + pick8(f64(vb), idx7, 64) * f64(eb)
    vcq = mxq(vc, 0, "e4m3")
    hidq = mxq(hid, 0, "e4m3")
    y = vcq.T @ hidq
    return y

@@ -1,0 +1,194 @@
+from contextlib import ExitStack
+
+import concourse.mybir as mybir
+
+F32 = mybir.dt.float32
+BF16 = mybir.dt.bfloat16
+I32 = mybir.dt.int32
+U32 = mybir.dt.uint32
+U16 = mybir.dt.uint16
+U8 = mybir.dt.uint8
+FP8X4 = mybir.dt.float8_e4m3fn_x4
+COPY = mybir.ActivationFunctionType.Copy
+MAX = mybir.AluOpType.max
+ADD = mybir.AluOpType.add
+XY = mybir.AxisListType.XY
+
+K, J, R, T, F, S, O, N, Z = 512, 512, 512, 1024, 1024, 256, 128, 256, 512
+P = 128
+PACK = 4
+HALF = J // 2
+FLOPS = 2 * K * R * J + 2 * R * N * O
+
+
+def tile_picked_largercode_store_one_pooledgroups_twobooks_plain_kernel(
+    tc, ta, tb, ga, gb, wt_words, wt_scales, sa, sb, va, vb, ea, eb,
+    offs, offs2, offs3, offs4, offs5, offs6, offs7, out,
+):
+    nc = tc.nc
+    with ExitStack() as ctx:
+        lists = ctx.enter_context(tc.tile_pool(name="lists", bufs=1))
+        keep = ctx.enter_context(tc.tile_pool(name="keep", bufs=1))
+        psum = ctx.enter_context(tc.psum_pool(name="psum", bufs=1))
+
+        def load_list(src, name):
+            tile = lists.tile([P, src.shape[1]], U16, name=name)
+            nc.sync.dma_start(tile[:], src)
+            return tile
+
+        def load_steps(queue, src, name):
+            tile = keep.tile([P, PACK], F32, name=name)
+            queue.dma_start(tile[:], src.rearrange("(p t) o -> p (t o)", t=PACK))
+            return tile
+
+        def load_plane(src, t, name):
+            tile = keep.tile([P, src.shape[1]], F32, name=name + str(t), tag=name + str(t))
+            nc.sync.dma_start(tile[:], src.rearrange("(p t) c -> p t c", t=PACK)[:, t, :])
+            return tile
+
+        def fetch(dst, window, offsets, step):
+            nc.scalar.activation(out=dst, in_=window[:].indirect(offsets), func=COPY, scale=step)
+
+        def combine(planes_a, planes_b, op, name, tag):
+            width = planes_a.shape[2]
+            grouped = keep.tile([P, width, PACK], BF16, name=name + "_grouped", tag=tag, align_bytes=64)
+            nc.vector.tensor_tensor(
+                out=grouped[:].rearrange("p (c i) t -> p c t i", i=4),
+                in0=planes_a.rearrange("p t (c i) -> p c t i", i=4),
+                in1=planes_b.rearrange("p t (c i) -> p c t i", i=4),
+                op=op,
+            )
+            return grouped
+
+        def quantize(grouped, name):
+            width = grouped.shape[1]
+            codes = keep.tile([P, width], U32, name=name + "_codes", tag=name + "_codes", align_bytes=64)
+            scales = keep.tile([P, width], U8, name=name + "_scales", align_bytes=64)
+            nc.vector.quantize_mx(
+                out=codes[:].bitcast(FP8X4), scales=scales[:],
+                in_=grouped[:].rearrange("p w t -> p (w t)"),
+            )
+            return codes, scales
+
+        ta_p, tb_p, va_p, vb_p = [], [], [], []
+        ta_p.append(load_plane(ta, 0, "ta"))
+        l_ta = load_list(offs, "l_ta")
+        ga_t = load_steps(nc.scalar, ga, "ga")
+        tb_p.append(load_plane(tb, 0, "tb"))
+        l_tb = load_list(offs2, "l_tb")
+        gb_t = load_steps(nc.scalar, gb, "gb")
+        scale_rows = keep.tile([4, 4, F], U8, name="scale_rows")
+        nc.gpsimd.dma_start(
+            scale_rows[:].bitcast(I32),
+            wt_scales[0].rearrange("(q i) c -> i q c", i=4).bitcast(I32),
+        )
+        ea_t = load_steps(nc.gpsimd, ea, "ea")
+        eb_t = load_steps(nc.gpsimd, eb, "eb")
+        sa_t = load_steps(nc.gpsimd, sa, "sa")
+        sb_t = load_steps(nc.gpsimd, sb, "sb")
+        ta_p.append(load_plane(ta, 1, "ta"))
+        tb_p.append(load_plane(tb, 1, "tb"))
+        ta_p.append(load_plane(ta, 2, "ta"))
+        l_wt = load_list(offs3, "l_wt")
+        tb_p.append(load_plane(tb, 2, "tb"))
+        l_va = load_list(offs6, "l_va")
+        ta_p.append(load_plane(ta, 3, "ta"))
+        l_vb = load_list(offs7, "l_vb")
+        word_window = keep.tile([P, F], I32, name="word_window")
+        nc.sync.dma_start(word_window[:], wt_words[0].rearrange("p c r -> p (c r)").bitcast(I32))
+        tb_p.append(load_plane(tb, 3, "tb"))
+        l_own = load_list(offs4, "l_own")
+        l_one = load_list(offs5, "l_one")
+        for t in range(PACK):
+            va_p.append(load_plane(va, t, "va"))
+            vb_p.append(load_plane(vb, t, "vb"))
+
+        scale_window = keep.tile([P, F], U8, name="scale_window")
+        nc.vector.memset(scale_window[:].bitcast(I32), 0)
+        for q in range(4):
+            nc.vector.tensor_copy(
+                out=scale_window[32 * q : 32 * q + 4, :].bitcast(I32),
+                in_=scale_rows[:, q, :].bitcast(I32),
+            )
+        w_scales = keep.tile([P, R], U8, name="w_scales", align_bytes=64)
+        nc.vector.tensor_copy(
+            out=w_scales[:].rearrange("p (t m) -> p m t", t=PACK),
+            in_=scale_window[:].indirect(l_wt[:]),
+        )
+
+        xa = keep.tile([P, PACK, J], F32, name="xa")
+        xb = keep.tile([P, PACK, J], F32, name="xb")
+        cols = HALF // 16
+        for t in range(PACK):
+            fetch(xa[:, t, :], ta_p[t], l_ta[:], ga_t[:, t : t + 1])
+            if t < PACK - 1:
+                fetch(xb[:, t, :], tb_p[t], l_tb[:], gb_t[:, t : t + 1])
+            else:
+                for h in range(2):
+                    fetch(xb[:, t, h * HALF : (h + 1) * HALF], tb_p[t], l_tb[:, h * cols : (h + 1) * cols], gb_t[:, t : t + 1])
+
+        w_codes = keep.tile([P, R], U32, name="w_codes", align_bytes=64)
+        nc.vector.tensor_copy(
+            out=w_codes[:].rearrange("p (t m) -> p m t", t=PACK),
+            in_=word_window[:].bitcast(U32).indirect(l_wt[:]),
+        )
+        x_grouped0 = combine(xa[:, :, :HALF], xb[:, :, :HALF], MAX, "x0", "x0_grouped")
+        x_q = [quantize(x_grouped0, "x0")]
+        x_grouped1 = combine(xa[:, :, HALF:], xb[:, :, HALF:], MAX, "x1", "x1_grouped")
+        x_q.append(quantize(x_grouped1, "x1"))
+
+        vca = keep.tile([P, PACK, N], F32, name="vca")
+        vcb = keep.tile([P, PACK, N], F32, name="vcb")
+        for t in range(PACK):
+            fetch(vca[:, t, :], va_p[t], l_va[:], ea_t[:, t : t + 1])
+            fetch(vcb[:, t, :], vb_p[t], l_vb[:], eb_t[:, t : t + 1])
+
+        a_bank = [psum.tile([P, J], F32, name="a_bank" + str(t)) for t in range(PACK)]
+        for h in range(2):
+            for t in range(PACK):
+                m_cols = slice(t * P, (t + 1) * P)
+                nc.tensor.matmul_mx(
+                    out=a_bank[t][:, h * HALF : (h + 1) * HALF],
+                    lhsT=w_codes[:, m_cols].bitcast(FP8X4), lhsT_scale=w_scales[:, m_cols],
+                    rhs=x_q[h][0][:].bitcast(FP8X4), rhs_scale=x_q[h][1][:],
+                    start=True, stop=True,
+                )
+        a_rows = []
+        for t in range(PACK):
+            a_t = keep.tile([P, J], F32, name="a_rows" + str(t))
+            nc.vector.tensor_copy(out=a_t[:], in_=a_bank[t][:])
+            a_rows.append(a_t)
+
+        v_grouped = combine(vca[:], vcb[:], ADD, "v", "x1_codes")
+        v_codes, v_scales = quantize(v_grouped, "v")
+
+        h_grouped = keep.tile([P, O, PACK], BF16, name="h_grouped", align_bytes=64)
+        spent = ["vb3", "va3", "vb2", "va2", "vb1"]
+        pieces = [(t, 0, S) for t in range(PACK - 1)] + [(PACK - 1, 0, S // 2), (PACK - 1, S // 2, S)]
+        for (t, s0, s1), tag in zip(pieces, spent):
+            picks = keep.tile([P, 2, s1 - s0], F32, name="picks", tag=tag)
+            fetch(picks[:, 0, :], a_rows[t], l_own[:, s0 // 16 : s1 // 16], sa_t[:, t : t + 1])
+            fetch(picks[:, 1, :], a_rows[t], l_one[:, s0 // 16 : s1 // 16], sb_t[:, t : t + 1])
+            nc.vector.tensor_reduce(
+                out=h_grouped[:, s0 // 2 : s1 // 2, t],
+                in_=picks[:].rearrange("p u (o d) -> p o u d", d=2),
+                axis=XY, op=MAX,
+            )
+        h_codes, h_scales = quantize(h_grouped, "h")
+
+        for b in range(N // P):
+            n_cols = slice(b * P, (b + 1) * P)
+            y_bank = psum.tile([P, O], F32, name="y_bank" + str(b))
+            nc.tensor.matmul_mx(
+                out=y_bank[:],
+                lhsT=v_codes[:, n_cols].bitcast(FP8X4), lhsT_scale=v_scales[:, n_cols],
+                rhs=h_codes[:].bitcast(FP8X4), rhs_scale=h_scales[:],
+                start=True, stop=True,
+            )
+            y_rows = keep.tile([P, O], F32, name="y_rows" + str(b))
+            if b == 0:
+                nc.vector.tensor_copy(out=y_rows[:], in_=y_bank[:])
+                nc.sync.dma_start(out[n_cols, :], y_rows[:])
+            else:
+                nc.scalar.copy(out=y_rows[:], in_=y_bank[:])
+                nc.scalar.dma_start(out[n_cols, :], y_rows[:])

@@ -53,9 +53,9 @@ def tile_picked_largercode_store_one_pooledgroups_twobooks_plain_kernel(
             width = planes_a.shape[2]
             grouped = keep.tile([P, width, PACK], BF16, name=name + "_grouped", tag=tag, align_bytes=64)
             nc.vector.tensor_tensor(
-                out=grouped[:].rearrange("p (c i) t -> p c t i", i=4),
-                in0=planes_a.rearrange("p t (c i) -> p c t i", i=4),
-                in1=planes_b.rearrange("p t (c i) -> p c t i", i=4),
+                out=grouped[:].rearrange("p (c i) t -> p c t i", i=2),
+                in0=planes_a.rearrange("p t (c i) -> p c t i", i=2),
+                in1=planes_b.rearrange("p t (c i) -> p c t i", i=2),
                 op=op,
             )
             return grouped
@@ -77,38 +77,39 @@ def tile_picked_largercode_store_one_pooledgroups_twobooks_plain_kernel(
         tb_p.append(load_plane(tb, 0, "tb"))
         l_tb = load_list(offs2, "l_tb")
         gb_t = load_steps(nc.scalar, gb, "gb")
-        scale_rows = keep.tile([4, 4, F], U8, name="scale_rows")
-        nc.gpsimd.dma_start(
-            scale_rows[:].bitcast(I32),
-            wt_scales[0].rearrange("(q i) c -> i q c", i=4).bitcast(I32),
-        )
-        ea_t = load_steps(nc.gpsimd, ea, "ea")
-        eb_t = load_steps(nc.gpsimd, eb, "eb")
-        sa_t = load_steps(nc.gpsimd, sa, "sa")
-        sb_t = load_steps(nc.gpsimd, sb, "sb")
+        scale_rows = keep.tile([P, 2, F], U8, name="scale_rows")
+        for u in range(2):
+            nc.gpsimd.dma_start(
+                scale_rows[64 * u : 64 * u + 4].bitcast(I32),
+                wt_scales[0, 8 * u : 8 * u + 8].rearrange("(q i) c -> i q c", i=4).bitcast(I32),
+            )
         ta_p.append(load_plane(ta, 1, "ta"))
         tb_p.append(load_plane(tb, 1, "tb"))
-        ta_p.append(load_plane(ta, 2, "ta"))
         l_wt = load_list(offs3, "l_wt")
-        tb_p.append(load_plane(tb, 2, "tb"))
-        l_va = load_list(offs6, "l_va")
-        ta_p.append(load_plane(ta, 3, "ta"))
-        l_vb = load_list(offs7, "l_vb")
         word_window = keep.tile([P, F], I32, name="word_window")
         nc.sync.dma_start(word_window[:], wt_words[0].rearrange("p c r -> p (c r)").bitcast(I32))
+        ta_p.append(load_plane(ta, 2, "ta"))
+        tb_p.append(load_plane(tb, 2, "tb"))
+        l_va = load_list(offs6, "l_va")
+        ea_t = load_steps(nc.sync, ea, "ea")
+        ta_p.append(load_plane(ta, 3, "ta"))
+        l_vb = load_list(offs7, "l_vb")
+        eb_t = load_steps(nc.sync, eb, "eb")
         tb_p.append(load_plane(tb, 3, "tb"))
-        l_own = load_list(offs4, "l_own")
-        l_one = load_list(offs5, "l_one")
         for t in range(PACK):
             va_p.append(load_plane(va, t, "va"))
             vb_p.append(load_plane(vb, t, "vb"))
+        l_own = load_list(offs4, "l_own")
+        sa_t = load_steps(nc.sync, sa, "sa")
+        l_one = load_list(offs5, "l_one")
+        sb_t = load_steps(nc.sync, sb, "sb")
 
         scale_window = keep.tile([P, F], U8, name="scale_window")
         nc.vector.memset(scale_window[:].bitcast(I32), 0)
         for q in range(4):
             nc.vector.tensor_copy(
                 out=scale_window[32 * q : 32 * q + 4, :].bitcast(I32),
-                in_=scale_rows[:, q, :].bitcast(I32),
+                in_=scale_rows[64 * (q // 2) : 64 * (q // 2) + 4, q % 2, :].bitcast(I32),
             )
         w_scales = keep.tile([P, R], U8, name="w_scales", align_bytes=64)
         nc.vector.tensor_copy(
@@ -116,25 +117,43 @@ def tile_picked_largercode_store_one_pooledgroups_twobooks_plain_kernel(
             in_=scale_window[:].indirect(l_wt[:]),
         )
 
-        xa = keep.tile([P, PACK, J], F32, name="xa")
-        xb = keep.tile([P, PACK, J], F32, name="xb")
-        cols = HALF // 16
-        for t in range(PACK):
-            fetch(xa[:, t, :], ta_p[t], l_ta[:], ga_t[:, t : t + 1])
-            if t < PACK - 1:
-                fetch(xb[:, t, :], tb_p[t], l_tb[:], gb_t[:, t : t + 1])
-            else:
-                for h in range(2):
-                    fetch(xb[:, t, h * HALF : (h + 1) * HALF], tb_p[t], l_tb[:, h * cols : (h + 1) * cols], gb_t[:, t : t + 1])
-
         w_codes = keep.tile([P, R], U32, name="w_codes", align_bytes=64)
         nc.vector.tensor_copy(
             out=w_codes[:].rearrange("p (t m) -> p m t", t=PACK),
             in_=word_window[:].bitcast(U32).indirect(l_wt[:]),
         )
-        x_grouped0 = combine(xa[:, :, :HALF], xb[:, :, :HALF], MAX, "x0", "x0_grouped")
+
+        xa = keep.tile([P, PACK, J], F32, name="xa")
+        xb = keep.tile([P, PACK, J], F32, name="xb")
+        x_planes = [keep.tile([P, PACK, HALF], BF16, name="x_planes" + str(h)) for h in range(2)]
+        cols = HALF // 16
+
+        def larger(t, h):
+            j_cols = slice(h * HALF, (h + 1) * HALF)
+            nc.vector.tensor_tensor(out=x_planes[h][:, t, :], in0=xa[:, t, j_cols], in1=xb[:, t, j_cols], op=MAX)
+
+        def weave(h):
+            grouped = keep.tile([P, HALF, PACK], BF16, name="x_grouped" + str(h), align_bytes=64)
+            nc.vector.tensor_copy(
+                out=grouped[:].rearrange("p (c i) t -> p c t i", i=4),
+                in_=x_planes[h][:].rearrange("p t (c i) -> p c t i", i=4),
+            )
+            return grouped
+
+        for t in range(PACK):
+            fetch(xa[:, t, :], ta_p[t], l_ta[:], ga_t[:, t : t + 1])
+            if t < PACK - 1:
+                fetch(xb[:, t, :], tb_p[t], l_tb[:], gb_t[:, t : t + 1])
+                larger(t, 0)
+                larger(t, 1)
+            else:
+                for h in range(2):
+                    fetch(xb[:, t, h * HALF : (h + 1) * HALF], tb_p[t], l_tb[:, h * cols : (h + 1) * cols], gb_t[:, t : t + 1])
+        larger(PACK - 1, 0)
+        x_grouped0 = weave(0)
+        larger(PACK - 1, 1)
         x_q = [quantize(x_grouped0, "x0")]
-        x_grouped1 = combine(xa[:, :, HALF:], xb[:, :, HALF:], MAX, "x1", "x1_grouped")
+        x_grouped1 = weave(1)
         x_q.append(quantize(x_grouped1, "x1"))
 
         vca = keep.tile([P, PACK, N], F32, name="vca")

@@ -77,6 +77,10 @@ def tile_picked_largercode_store_one_pooledgroups_twobooks_plain_kernel(
         tb_p.append(load_plane(tb, 0, "tb"))
         l_tb = load_list(offs2, "l_tb")
         gb_t = load_steps(nc.scalar, gb, "gb")
+        warm_in = keep.tile([P, 1], F32, name="warm_in")
+        warm_out = keep.tile([P, 1], F32, name="warm_out")
+        nc.vector.memset(warm_in[:], 0.0)
+        nc.scalar.activation(out=warm_out[:], in_=warm_in[:], func=COPY)
         scale_rows = keep.tile([P, 2, F], U8, name="scale_rows")
         for u in range(2):
             nc.gpsimd.dma_start(

@@ -14,10 +14,14 @@ MAX = mybir.AluOpType.max
 ADD = mybir.AluOpType.add
 XY = mybir.AxisListType.XY
 
-K, J, R, T, F, S, O, N, Z = 512, 512, 512, 1024, 1024, 256, 128, 256, 512
+K, J, R, F, S, O, N = 512, 512, 512, 1024, 256, 128, 256
 P = 128
 PACK = 4
+LAST = PACK - 1
+ENTRIES = 16
 HALF = J // 2
+QUADRANT = 32
+SPLIT_PLANES = 2
 FLOPS = 2 * K * R * J + 2 * R * N * O
 
 
@@ -36,7 +40,7 @@ def tile_picked_largercode_store_one_pooledgroups_twobooks_plain_kernel(
             nc.sync.dma_start(tile[:], src)
             return tile
 
-        def load_steps(queue, src, name):
+        def load_factors(queue, src, name):
             tile = keep.tile([P, PACK], F32, name=name)
             queue.dma_start(tile[:], src.rearrange("(p t) o -> p (t o)", t=PACK))
             return tile
@@ -46,19 +50,9 @@ def tile_picked_largercode_store_one_pooledgroups_twobooks_plain_kernel(
             nc.sync.dma_start(tile[:], src.rearrange("(p t) c -> p t c", t=PACK)[:, t, :])
             return tile
 
-        def fetch(dst, window, offsets, step):
-            nc.scalar.activation(out=dst, in_=window[:].indirect(offsets), func=COPY, scale=step)
-
-        def combine(planes_a, planes_b, op, name, tag):
-            width = planes_a.shape[2]
-            grouped = keep.tile([P, width, PACK], BF16, name=name + "_grouped", tag=tag, align_bytes=64)
-            nc.vector.tensor_tensor(
-                out=grouped[:].rearrange("p (c i) t -> p c t i", i=2),
-                in0=planes_a.rearrange("p t (c i) -> p c t i", i=2),
-                in1=planes_b.rearrange("p t (c i) -> p c t i", i=2),
-                op=op,
-            )
-            return grouped
+        def fetch(dst, window, offsets, first, end, factor):
+            entries = offsets[:, first // ENTRIES : end // ENTRIES]
+            nc.scalar.activation(out=dst, in_=window[:].indirect(entries), func=COPY, scale=factor)
 
         def quantize(grouped, name):
             width = grouped.shape[1]
@@ -66,152 +60,161 @@ def tile_picked_largercode_store_one_pooledgroups_twobooks_plain_kernel(
             scales = keep.tile([P, width], U8, name=name + "_scales", align_bytes=64)
             nc.vector.quantize_mx(
                 out=codes[:].bitcast(FP8X4), scales=scales[:],
-                in_=grouped[:].rearrange("p w t -> p (w t)"),
+                in_=grouped[:].rearrange("p c t -> p (c t)"),
             )
             return codes, scales
 
-        ta_p, tb_p, va_p, vb_p = [], [], [], []
-        ta_p.append(load_plane(ta, 0, "ta"))
-        l_ta = load_list(offs, "l_ta")
-        ga_t = load_steps(nc.scalar, ga, "ga")
-        tb_p.append(load_plane(tb, 0, "tb"))
-        l_tb = load_list(offs2, "l_tb")
-        gb_t = load_steps(nc.scalar, gb, "gb")
+        ta_planes = [load_plane(ta, 0, "ta")]
+        ta_list = load_list(offs, "ta_list")
+        ga_cols = load_factors(nc.scalar, ga, "ga")
+        tb_planes = [load_plane(tb, 0, "tb")]
+        tb_list = load_list(offs2, "tb_list")
+        gb_cols = load_factors(nc.scalar, gb, "gb")
+
         warm_in = keep.tile([P, 1], F32, name="warm_in")
         warm_out = keep.tile([P, 1], F32, name="warm_out")
         nc.vector.memset(warm_in[:], 0.0)
         nc.scalar.activation(out=warm_out[:], in_=warm_in[:], func=COPY)
+
         scale_rows = keep.tile([P, 2, F], U8, name="scale_rows")
         for u in range(2):
             nc.gpsimd.dma_start(
-                scale_rows[64 * u : 64 * u + 4].bitcast(I32),
-                wt_scales[0, 8 * u : 8 * u + 8].rearrange("(q i) c -> i q c", i=4).bitcast(I32),
+                scale_rows[2 * QUADRANT * u : 2 * QUADRANT * u + 4].bitcast(I32),
+                wt_scales[0, 8 * u : 8 * u + 8].rearrange("(v i) c -> i v c", i=4).bitcast(I32),
             )
-        ta_p.append(load_plane(ta, 1, "ta"))
-        tb_p.append(load_plane(tb, 1, "tb"))
-        l_wt = load_list(offs3, "l_wt")
+        ta_planes.append(load_plane(ta, 1, "ta"))
+        tb_planes.append(load_plane(tb, 1, "tb"))
+        wt_list = load_list(offs3, "wt_list")
+        for t in range(2, PACK):
+            ta_planes.append(load_plane(ta, t, "ta"))
+            tb_planes.append(load_plane(tb, t, "tb"))
         word_window = keep.tile([P, F], I32, name="word_window")
         nc.sync.dma_start(word_window[:], wt_words[0].rearrange("p c r -> p (c r)").bitcast(I32))
-        ta_p.append(load_plane(ta, 2, "ta"))
-        tb_p.append(load_plane(tb, 2, "tb"))
-        l_va = load_list(offs6, "l_va")
-        ea_t = load_steps(nc.sync, ea, "ea")
-        ta_p.append(load_plane(ta, 3, "ta"))
-        l_vb = load_list(offs7, "l_vb")
-        eb_t = load_steps(nc.sync, eb, "eb")
-        tb_p.append(load_plane(tb, 3, "tb"))
-        for t in range(PACK):
-            va_p.append(load_plane(va, t, "va"))
-            vb_p.append(load_plane(vb, t, "vb"))
-        l_own = load_list(offs4, "l_own")
-        sa_t = load_steps(nc.sync, sa, "sa")
-        l_one = load_list(offs5, "l_one")
-        sb_t = load_steps(nc.sync, sb, "sb")
+        va_list = load_list(offs6, "va_list")
+        ea_cols = load_factors(nc.sync, ea, "ea")
+        va_planes = [load_plane(va, 0, "va")]
+        vb_list = load_list(offs7, "vb_list")
+        eb_cols = load_factors(nc.sync, eb, "eb")
+        vb_planes = [load_plane(vb, 0, "vb")]
+        for t in range(1, PACK):
+            va_planes.append(load_plane(va, t, "va"))
+            vb_planes.append(load_plane(vb, t, "vb"))
+        own_list = load_list(offs4, "own_list")
+        sa_cols = load_factors(nc.sync, sa, "sa")
+        shared_list = load_list(offs5, "shared_list")
+        sb_cols = load_factors(nc.sync, sb, "sb")
 
         scale_window = keep.tile([P, F], U8, name="scale_window")
         nc.vector.memset(scale_window[:].bitcast(I32), 0)
-        for q in range(4):
+        for q in range(P // QUADRANT):
+            u, v = divmod(q, 2)
             nc.vector.tensor_copy(
-                out=scale_window[32 * q : 32 * q + 4, :].bitcast(I32),
-                in_=scale_rows[64 * (q // 2) : 64 * (q // 2) + 4, q % 2, :].bitcast(I32),
+                out=scale_window[QUADRANT * q : QUADRANT * q + 4, :].bitcast(I32),
+                in_=scale_rows[2 * QUADRANT * u : 2 * QUADRANT * u + 4, v, :].bitcast(I32),
             )
         w_scales = keep.tile([P, R], U8, name="w_scales", align_bytes=64)
         nc.vector.tensor_copy(
             out=w_scales[:].rearrange("p (t m) -> p m t", t=PACK),
-            in_=scale_window[:].indirect(l_wt[:]),
+            in_=scale_window[:].indirect(wt_list[:]),
         )
-
         w_codes = keep.tile([P, R], U32, name="w_codes", align_bytes=64)
         nc.vector.tensor_copy(
             out=w_codes[:].rearrange("p (t m) -> p m t", t=PACK),
-            in_=word_window[:].bitcast(U32).indirect(l_wt[:]),
+            in_=word_window[:].bitcast(U32).indirect(wt_list[:]),
         )
 
         xa = keep.tile([P, PACK, J], F32, name="xa")
         xb = keep.tile([P, PACK, J], F32, name="xb")
-        x_planes = [keep.tile([P, PACK, HALF], BF16, name="x_planes" + str(h)) for h in range(2)]
-        cols = HALF // 16
+        x_planes = [keep.tile([P, PACK, HALF], BF16, name="x_planes" + str(half)) for half in range(2)]
 
-        def larger(t, h):
-            j_cols = slice(h * HALF, (h + 1) * HALF)
-            nc.vector.tensor_tensor(out=x_planes[h][:, t, :], in0=xa[:, t, j_cols], in1=xb[:, t, j_cols], op=MAX)
+        def larger(t, half):
+            slots = slice(half * HALF, (half + 1) * HALF)
+            nc.vector.tensor_tensor(out=x_planes[half][:, t, :], in0=xa[:, t, slots], in1=xb[:, t, slots], op=MAX)
 
-        def weave(h):
-            grouped = keep.tile([P, HALF, PACK], BF16, name="x_grouped" + str(h), align_bytes=64)
+        def interleave(half):
+            grouped = keep.tile([P, HALF, PACK], BF16, name="x_grouped" + str(half), align_bytes=64)
             nc.vector.tensor_copy(
                 out=grouped[:].rearrange("p (c i) t -> p c t i", i=4),
-                in_=x_planes[h][:].rearrange("p t (c i) -> p c t i", i=4),
+                in_=x_planes[half][:].rearrange("p t (c i) -> p c t i", i=4),
             )
             return grouped
 
-        for t in range(PACK):
-            fetch(xa[:, t, :], ta_p[t], l_ta[:], ga_t[:, t : t + 1])
-            if t < PACK - 1:
-                fetch(xb[:, t, :], tb_p[t], l_tb[:], gb_t[:, t : t + 1])
-                larger(t, 0)
-                larger(t, 1)
-            else:
-                for h in range(2):
-                    fetch(xb[:, t, h * HALF : (h + 1) * HALF], tb_p[t], l_tb[:, h * cols : (h + 1) * cols], gb_t[:, t : t + 1])
-        larger(PACK - 1, 0)
-        x_grouped0 = weave(0)
-        larger(PACK - 1, 1)
-        x_q = [quantize(x_grouped0, "x0")]
-        x_grouped1 = weave(1)
-        x_q.append(quantize(x_grouped1, "x1"))
+        for t in range(LAST):
+            fetch(xa[:, t, :], ta_planes[t], ta_list, 0, J, ga_cols[:, t : t + 1])
+            fetch(xb[:, t, :], tb_planes[t], tb_list, 0, J, gb_cols[:, t : t + 1])
+            larger(t, 0)
+            larger(t, 1)
+        fetch(xa[:, LAST, :], ta_planes[LAST], ta_list, 0, J, ga_cols[:, LAST:])
+        fetch(xb[:, LAST, :HALF], tb_planes[LAST], tb_list, 0, HALF, gb_cols[:, LAST:])
+        fetch(xb[:, LAST, HALF:], tb_planes[LAST], tb_list, HALF, J, gb_cols[:, LAST:])
+        larger(LAST, 0)
+        x_grouped0 = interleave(0)
+        larger(LAST, 1)
+        x_halves = [quantize(x_grouped0, "x0")]
+        x_grouped1 = interleave(1)
+        x_halves.append(quantize(x_grouped1, "x1"))
 
         vca = keep.tile([P, PACK, N], F32, name="vca")
         vcb = keep.tile([P, PACK, N], F32, name="vcb")
         for t in range(PACK):
-            fetch(vca[:, t, :], va_p[t], l_va[:], ea_t[:, t : t + 1])
-            fetch(vcb[:, t, :], vb_p[t], l_vb[:], eb_t[:, t : t + 1])
+            fetch(vca[:, t, :], va_planes[t], va_list, 0, N, ea_cols[:, t : t + 1])
+            fetch(vcb[:, t, :], vb_planes[t], vb_list, 0, N, eb_cols[:, t : t + 1])
 
-        a_bank = [psum.tile([P, J], F32, name="a_bank" + str(t)) for t in range(PACK)]
-        for h in range(2):
+        a_planes = [keep.tile([P, J], F32, name="a_plane" + str(t)) for t in range(PACK)]
+        half_banks = [
+            [psum.tile([P, HALF], F32, name="a_half" + str(t) + str(half)) for half in range(2)]
+            for t in range(SPLIT_PLANES)
+        ]
+        whole_banks = {t: psum.tile([P, J], F32, name="a_bank" + str(t)) for t in range(SPLIT_PLANES, PACK)}
+        for half in range(2):
+            slots = slice(half * HALF, (half + 1) * HALF)
+            x_codes, x_scales = x_halves[half]
             for t in range(PACK):
-                m_cols = slice(t * P, (t + 1) * P)
+                plane_cols = slice(t * P, (t + 1) * P)
                 nc.tensor.matmul_mx(
-                    out=a_bank[t][:, h * HALF : (h + 1) * HALF],
-                    lhsT=w_codes[:, m_cols].bitcast(FP8X4), lhsT_scale=w_scales[:, m_cols],
-                    rhs=x_q[h][0][:].bitcast(FP8X4), rhs_scale=x_q[h][1][:],
+                    out=half_banks[t][half][:] if t < SPLIT_PLANES else whole_banks[t][:, slots],
+                    lhsT=w_codes[:, plane_cols].bitcast(FP8X4), lhsT_scale=w_scales[:, plane_cols],
+                    rhs=x_codes[:].bitcast(FP8X4), rhs_scale=x_scales[:],
                     start=True, stop=True,
                 )
-        a_rows = []
-        for t in range(PACK):
-            a_t = keep.tile([P, J], F32, name="a_rows" + str(t))
-            nc.vector.tensor_copy(out=a_t[:], in_=a_bank[t][:])
-            a_rows.append(a_t)
+            for t in range(SPLIT_PLANES):
+                nc.vector.tensor_copy(out=a_planes[t][:, slots], in_=half_banks[t][half][:])
+        for t in range(SPLIT_PLANES, PACK):
+            nc.vector.tensor_copy(out=a_planes[t][:], in_=whole_banks[t][:])
 
-        v_grouped = combine(vca[:], vcb[:], ADD, "v", "x1_codes")
+        v_grouped = keep.tile([P, N, PACK], BF16, name="v_grouped", tag="x1_codes", align_bytes=64)
+        nc.vector.tensor_tensor(
+            out=v_grouped[:].rearrange("p (c i) t -> p c t i", i=2),
+            in0=vca[:].rearrange("p t (c i) -> p c t i", i=2),
+            in1=vcb[:].rearrange("p t (c i) -> p c t i", i=2),
+            op=ADD,
+        )
         v_codes, v_scales = quantize(v_grouped, "v")
 
         h_grouped = keep.tile([P, O, PACK], BF16, name="h_grouped", align_bytes=64)
-        spent = ["vb3", "va3", "vb2", "va2", "vb1"]
-        pieces = [(t, 0, S) for t in range(PACK - 1)] + [(PACK - 1, 0, S // 2), (PACK - 1, S // 2, S)]
-        for (t, s0, s1), tag in zip(pieces, spent):
-            picks = keep.tile([P, 2, s1 - s0], F32, name="picks", tag=tag)
-            fetch(picks[:, 0, :], a_rows[t], l_own[:, s0 // 16 : s1 // 16], sa_t[:, t : t + 1])
-            fetch(picks[:, 1, :], a_rows[t], l_one[:, s0 // 16 : s1 // 16], sb_t[:, t : t + 1])
+        spent = [name + str(t) for t in reversed(range(PACK)) for name in ("vb", "va")]
+        pieces = [(t, 0, S) for t in range(LAST)] + [(LAST, 0, S // 2), (LAST, S // 2, S)]
+        for (t, first, end), spent_tag in zip(pieces, spent):
+            picks = keep.tile([P, 2, end - first], F32, name="picks", tag=spent_tag)
+            fetch(picks[:, 0, :], a_planes[t], own_list, first, end, sa_cols[:, t : t + 1])
+            fetch(picks[:, 1, :], a_planes[t], shared_list, first, end, sb_cols[:, t : t + 1])
             nc.vector.tensor_reduce(
-                out=h_grouped[:, s0 // 2 : s1 // 2, t],
-                in_=picks[:].rearrange("p u (o d) -> p o u d", d=2),
+                out=h_grouped[:, first // 2 : end // 2, t],
+                in_=picks[:].rearrange("p side (o pair) -> p o side pair", pair=2),
                 axis=XY, op=MAX,
             )
         h_codes, h_scales = quantize(h_grouped, "h")
 
-        for b in range(N // P):
-            n_cols = slice(b * P, (b + 1) * P)
-            y_bank = psum.tile([P, O], F32, name="y_bank" + str(b))
+        ways_out = [(nc.vector.tensor_copy, nc.sync), (nc.scalar.copy, nc.scalar)]
+        for block, (copy_out, queue) in enumerate(ways_out):
+            rows = slice(block * P, (block + 1) * P)
+            y_bank = psum.tile([P, O], F32, name="y_bank" + str(block))
             nc.tensor.matmul_mx(
                 out=y_bank[:],
-                lhsT=v_codes[:, n_cols].bitcast(FP8X4), lhsT_scale=v_scales[:, n_cols],
+                lhsT=v_codes[:, rows].bitcast(FP8X4), lhsT_scale=v_scales[:, rows],
                 rhs=h_codes[:].bitcast(FP8X4), rhs_scale=h_scales[:],
                 start=True, stop=True,
             )
-            y_rows = keep.tile([P, O], F32, name="y_rows" + str(b))
-            if b == 0:
-                nc.vector.tensor_copy(out=y_rows[:], in_=y_bank[:])
-                nc.sync.dma_start(out[n_cols, :], y_rows[:])
-            else:
-                nc.scalar.copy(out=y_rows[:], in_=y_bank[:])
-                nc.scalar.dma_start(out[n_cols, :], y_rows[:])
+            y_rows = keep.tile([P, O], F32, name="y_rows" + str(block))
+            copy_out(out=y_rows[:], in_=y_bank[:])
+            queue.dma_start(out[rows, :], y_rows[:])

from contextlib import ExitStack

import concourse.mybir as mybir

F32 = mybir.dt.float32
BF16 = mybir.dt.bfloat16
I32 = mybir.dt.int32
U32 = mybir.dt.uint32
U16 = mybir.dt.uint16
U8 = mybir.dt.uint8
FP8X4 = mybir.dt.float8_e4m3fn_x4
COPY = mybir.ActivationFunctionType.Copy
MAX = mybir.AluOpType.max
ADD = mybir.AluOpType.add
XY = mybir.AxisListType.XY

K, J, R, F, S, O, N = 512, 512, 512, 1024, 256, 128, 256
P = 128
PACK = 4
LAST = PACK - 1
ENTRIES = 16
HALF = J // 2
QUADRANT = 32
SPLIT_PLANES = 2
FLOPS = 2 * K * R * J + 2 * R * N * O


def tile_picked_largercode_store_one_pooledgroups_twobooks_plain_kernel(
    tc, ta, tb, ga, gb, wt_words, wt_scales, sa, sb, va, vb, ea, eb,
    offs, offs2, offs3, offs4, offs5, offs6, offs7, out,
):
    nc = tc.nc
    with ExitStack() as ctx:
        lists = ctx.enter_context(tc.tile_pool(name="lists", bufs=1))
        keep = ctx.enter_context(tc.tile_pool(name="keep", bufs=1))
        psum = ctx.enter_context(tc.psum_pool(name="psum", bufs=1))

        def load_list(src, name):
            tile = lists.tile([P, src.shape[1]], U16, name=name)
            nc.sync.dma_start(tile[:], src)
            return tile

        def load_factors(queue, src, name):
            tile = keep.tile([P, PACK], F32, name=name)
            queue.dma_start(tile[:], src.rearrange("(p t) o -> p (t o)", t=PACK))
            return tile

        def load_plane(src, t, name):
            tile = keep.tile([P, src.shape[1]], F32, name=name + str(t), tag=name + str(t))
            nc.sync.dma_start(tile[:], src.rearrange("(p t) c -> p t c", t=PACK)[:, t, :])
            return tile

        def fetch(dst, window, offsets, first, end, factor):
            entries = offsets[:, first // ENTRIES : end // ENTRIES]
            nc.scalar.activation(out=dst, in_=window[:].indirect(entries), func=COPY, scale=factor)

        def quantize(grouped, name):
            width = grouped.shape[1]
            codes = keep.tile([P, width], U32, name=name + "_codes", tag=name + "_codes", align_bytes=64)
            scales = keep.tile([P, width], U8, name=name + "_scales", align_bytes=64)
            nc.vector.quantize_mx(
                out=codes[:].bitcast(FP8X4), scales=scales[:],
                in_=grouped[:].rearrange("p c t -> p (c t)"),
            )
            return codes, scales

        ta_planes = [load_plane(ta, 0, "ta")]
        ta_list = load_list(offs, "ta_list")
        ga_cols = load_factors(nc.scalar, ga, "ga")
        tb_planes = [load_plane(tb, 0, "tb")]
        tb_list = load_list(offs2, "tb_list")
        gb_cols = load_factors(nc.scalar, gb, "gb")

        warm_in = keep.tile([P, 1], F32, name="warm_in")
        warm_out = keep.tile([P, 1], F32, name="warm_out")
        nc.vector.memset(warm_in[:], 0.0)
        nc.scalar.activation(out=warm_out[:], in_=warm_in[:], func=COPY)

        scale_rows = keep.tile([P, 2, F], U8, name="scale_rows")
        for u in range(2):
            nc.gpsimd.dma_start(
                scale_rows[2 * QUADRANT * u : 2 * QUADRANT * u + 4].bitcast(I32),
                wt_scales[0, 8 * u : 8 * u + 8].rearrange("(v i) c -> i v c", i=4).bitcast(I32),
            )
        ta_planes.append(load_plane(ta, 1, "ta"))
        tb_planes.append(load_plane(tb, 1, "tb"))
        wt_list = load_list(offs3, "wt_list")
        for t in range(2, PACK):
            ta_planes.append(load_plane(ta, t, "ta"))
            tb_planes.append(load_plane(tb, t, "tb"))
        word_window = keep.tile([P, F], I32, name="word_window")
        nc.sync.dma_start(word_window[:], wt_words[0].rearrange("p c r -> p (c r)").bitcast(I32))
        va_list = load_list(offs6, "va_list")
        ea_cols = load_factors(nc.sync, ea, "ea")
        va_planes = [load_plane(va, 0, "va")]
        vb_list = load_list(offs7, "vb_list")
        eb_cols = load_factors(nc.sync, eb, "eb")
        vb_planes = [load_plane(vb, 0, "vb")]
        for t in range(1, PACK):
            va_planes.append(load_plane(va, t, "va"))
            vb_planes.append(load_plane(vb, t, "vb"))
        own_list = load_list(offs4, "own_list")
        sa_cols = load_factors(nc.sync, sa, "sa")
        shared_list = load_list(offs5, "shared_list")
        sb_cols = load_factors(nc.sync, sb, "sb")

        scale_window = keep.tile([P, F], U8, name="scale_window")
        nc.vector.memset(scale_window[:].bitcast(I32), 0)
        for q in range(P // QUADRANT):
            u, v = divmod(q, 2)
            nc.vector.tensor_copy(
                out=scale_window[QUADRANT * q : QUADRANT * q + 4, :].bitcast(I32),
                in_=scale_rows[2 * QUADRANT * u : 2 * QUADRANT * u + 4, v, :].bitcast(I32),
            )
        w_scales = keep.tile([P, R], U8, name="w_scales", align_bytes=64)
        nc.vector.tensor_copy(
            out=w_scales[:].rearrange("p (t m) -> p m t", t=PACK),
            in_=scale_window[:].indirect(wt_list[:]),
        )
        w_codes = keep.tile([P, R], U32, name="w_codes", align_bytes=64)
        nc.vector.tensor_copy(
            out=w_codes[:].rearrange("p (t m) -> p m t", t=PACK),
            in_=word_window[:].bitcast(U32).indirect(wt_list[:]),
        )

        xa = keep.tile([P, PACK, J], F32, name="xa")
        xb = keep.tile([P, PACK, J], F32, name="xb")
        x_planes = [keep.tile([P, PACK, HALF], BF16, name="x_planes" + str(half)) for half in range(2)]

        def larger(t, half):
            slots = slice(half * HALF, (half + 1) * HALF)
            nc.vector.tensor_tensor(out=x_planes[half][:, t, :], in0=xa[:, t, slots], in1=xb[:, t, slots], op=MAX)

        def interleave(half):
            grouped = keep.tile([P, HALF, PACK], BF16, name="x_grouped" + str(half), align_bytes=64)
            nc.vector.tensor_copy(
                out=grouped[:].rearrange("p (c i) t -> p c t i", i=4),
                in_=x_planes[half][:].rearrange("p t (c i) -> p c t i", i=4),
            )
            return grouped

        for t in range(LAST):
            fetch(xa[:, t, :], ta_planes[t], ta_list, 0, J, ga_cols[:, t : t + 1])
            fetch(xb[:, t, :], tb_planes[t], tb_list, 0, J, gb_cols[:, t : t + 1])
            larger(t, 0)
            larger(t, 1)
        fetch(xa[:, LAST, :], ta_planes[LAST], ta_list, 0, J, ga_cols[:, LAST:])
        fetch(xb[:, LAST, :HALF], tb_planes[LAST], tb_list, 0, HALF, gb_cols[:, LAST:])
        fetch(xb[:, LAST, HALF:], tb_planes[LAST], tb_list, HALF, J, gb_cols[:, LAST:])
        larger(LAST, 0)
        x_grouped0 = interleave(0)
        larger(LAST, 1)
        x_halves = [quantize(x_grouped0, "x0")]
        x_grouped1 = interleave(1)
        x_halves.append(quantize(x_grouped1, "x1"))

        vca = keep.tile([P, PACK, N], F32, name="vca")
        vcb = keep.tile([P, PACK, N], F32, name="vcb")
        for t in range(PACK):
            fetch(vca[:, t, :], va_planes[t], va_list, 0, N, ea_cols[:, t : t + 1])
            fetch(vcb[:, t, :], vb_planes[t], vb_list, 0, N, eb_cols[:, t : t + 1])

        a_planes = [keep.tile([P, J], F32, name="a_plane" + str(t)) for t in range(PACK)]
        half_banks = [
            [psum.tile([P, HALF], F32, name="a_half" + str(t) + str(half)) for half in range(2)]
            for t in range(SPLIT_PLANES)
        ]
        whole_banks = {t: psum.tile([P, J], F32, name="a_bank" + str(t)) for t in range(SPLIT_PLANES, PACK)}
        for half in range(2):
            slots = slice(half * HALF, (half + 1) * HALF)
            x_codes, x_scales = x_halves[half]
            for t in range(PACK):
                plane_cols = slice(t * P, (t + 1) * P)
                nc.tensor.matmul_mx(
                    out=half_banks[t][half][:] if t < SPLIT_PLANES else whole_banks[t][:, slots],
                    lhsT=w_codes[:, plane_cols].bitcast(FP8X4), lhsT_scale=w_scales[:, plane_cols],
                    rhs=x_codes[:].bitcast(FP8X4), rhs_scale=x_scales[:],
                    start=True, stop=True,
                )
            for t in range(SPLIT_PLANES):
                nc.vector.tensor_copy(out=a_planes[t][:, slots], in_=half_banks[t][half][:])
        for t in range(SPLIT_PLANES, PACK):
            nc.vector.tensor_copy(out=a_planes[t][:], in_=whole_banks[t][:])

        v_grouped = keep.tile([P, N, PACK], BF16, name="v_grouped", tag="x1_codes", align_bytes=64)
        nc.vector.tensor_tensor(
            out=v_grouped[:].rearrange("p (c i) t -> p c t i", i=2),
            in0=vca[:].rearrange("p t (c i) -> p c t i", i=2),
            in1=vcb[:].rearrange("p t (c i) -> p c t i", i=2),
            op=ADD,
        )
        v_codes, v_scales = quantize(v_grouped, "v")

        h_grouped = keep.tile([P, O, PACK], BF16, name="h_grouped", align_bytes=64)
        spent = [name + str(t) for t in reversed(range(PACK)) for name in ("vb", "va")]
        pieces = [(t, 0, S) for t in range(LAST)] + [(LAST, 0, S // 2), (LAST, S // 2, S)]
        for (t, first, end), spent_tag in zip(pieces, spent):
            picks = keep.tile([P, 2, end - first], F32, name="picks", tag=spent_tag)
            fetch(picks[:, 0, :], a_planes[t], own_list, first, end, sa_cols[:, t : t + 1])
            fetch(picks[:, 1, :], a_planes[t], shared_list, first, end, sb_cols[:, t : t + 1])
            nc.vector.tensor_reduce(
                out=h_grouped[:, first // 2 : end // 2, t],
                in_=picks[:].rearrange("p side (o pair) -> p o side pair", pair=2),
                axis=XY, op=MAX,
            )
        h_codes, h_scales = quantize(h_grouped, "h")

        ways_out = [(nc.vector.tensor_copy, nc.sync), (nc.scalar.copy, nc.scalar)]
        for block, (copy_out, queue) in enumerate(ways_out):
            rows = slice(block * P, (block + 1) * P)
            y_bank = psum.tile([P, O], F32, name="y_bank" + str(block))
            nc.tensor.matmul_mx(
                out=y_bank[:],
                lhsT=v_codes[:, rows].bitcast(FP8X4), lhsT_scale=v_scales[:, rows],
                rhs=h_codes[:].bitcast(FP8X4), rhs_scale=h_scales[:],
                start=True, stop=True,
            )
            y_rows = keep.tile([P, O], F32, name="y_rows" + str(block))
            copy_out(out=y_rows[:], in_=y_bank[:])
            queue.dma_start(out[rows, :], y_rows[:])
